import numpy as np
import ml_dtypes


def mxq(x, axis, fmt="e4m3"):
    dtype, down = {"e4m3": (ml_dtypes.float8_e4m3fn, 7), "e5m2": (ml_dtypes.float8_e5m2, 14)}[fmt]
    v = np.moveaxis(np.asarray(x, np.float32).astype(ml_dtypes.bfloat16).astype(np.float64), axis, -1)
    blocks = v.reshape(v.shape[:-1] + (-1, 32))
    amax = np.abs(blocks).max(-1, keepdims=True)
    byte = np.maximum(np.where(amax > 0, np.frexp(amax)[1] - 1 + 127, 0) - down, 1)
    scale = np.exp2(byte - 127.0)
    codes = (blocks / scale).astype(np.float32).astype(dtype).astype(np.float64)
    return np.moveaxis((codes * scale).reshape(v.shape), -1, axis)


WIDE = False


def mx_kscale(k):
    if not WIDE:
        return np.ones(k)
    levels = np.array([10, -10, 5, -5, 0])
    if k % 512:
        return np.exp2(np.random.permutation(np.resize(levels, k // 32))).repeat(32)
    a = np.empty((k // 512, 16))
    for p in range(k // 512):
        a[p, :8] = np.random.permutation(np.resize(levels, 8))
        for g in range(8):
            far = levels[np.abs(levels - a[p, g]) >= 10]
            a[p, g + 8] = far[np.random.randint(len(far))]
    return np.exp2(a.ravel()).repeat(32)


def f64(x):
    return np.asarray(x).astype(np.float64)


def striped(idx):
    return np.tile(idx.reshape(-1, 16).T, (8, 1)).astype(np.uint16)


def unstriped(offs):
    return offs[:16].T.reshape(-1).astype(np.int64)


def striped8(idx):
    return np.concatenate([x.reshape(-1, 16).T for x in idx]).astype(np.uint16)


def runs(offs, k):
    lists = np.stack([offs[16 * r : 16 * r + 16].T.reshape(-1) for r in range(8)]).astype(np.int64)
    return lists[np.arange(k) % 512 // 64]


def pack_weight(w):
    k, n = w.shape
    w = f64(np.asarray(w, np.float32).astype(ml_dtypes.bfloat16)).reshape(k // 32, 32, n)
    amax = np.abs(w).max(1)
    byte = np.clip(np.where(amax > 0, np.frexp(amax)[1] - 1 + 127 - 7, 1), 1, 254)
    scaled = (w * np.exp2(127.0 - byte)[:, None, :]).reshape(k, n).astype(np.float32)
    words = np.ascontiguousarray(scaled.reshape(k // 512, 128, 4, n).transpose(0, 1, 3, 2)).astype(ml_dtypes.float8_e4m3fn).view(np.uint8)
    return words, np.ascontiguousarray(byte.astype(np.uint8).reshape(k // 512, 16, n))


def unpack_weight(words, scales):
    g, p, n, _ = words.shape
    vals = np.ascontiguousarray(words).view(ml_dtypes.float8_e4m3fn).astype(np.float64) * np.repeat(np.exp2(scales.astype(np.float64) - 127.0), 8, axis=1)[..., None]
    return vals.transpose(0, 1, 3, 2).reshape(g * 512, n)


K, T, S, V, N, H = 512, 2048, 512, 256, 512, 512


def setup_inputs():
    n = np.random.standard_normal
    s = mx_kscale(K)[:, None]
    u = mx_kscale(H)
    packed_xT = pack_weight(n((K, T)) * s)
    return {
        "x_words": packed_xT[0],
        "x_scales": packed_xT[1],
        "w1": (n((K, H)) / np.sqrt(K) / s).astype(np.float32),
        "rest": np.random.uniform(0.2, 1.0, (H, V)).astype(np.float32),
        "gn": (np.random.uniform(0.5, 1.5, (H, 1)) * u[:, None]).astype(np.float32),
        "w2": (n((H, N)) / np.sqrt(H) / u[:, None]).astype(np.float32),
        "offs": striped(np.random.permutation(T)[:S]),
        "a_l": striped8(np.stack([np.random.permutation(S)[:V] for _ in range(8)])),
        "b_l": striped8(np.stack([np.random.permutation(S)[:V] for _ in range(8)])),
    }


def reference(x_words, x_scales, w1, rest, gn, w2, offs, a_l, b_l):
    xq = unpack_weight(x_words, x_scales)[:, unstriped(offs)]
    y = mxq(f64(w1), 0, "e4m3").T @ xq
    d = y[np.arange(H)[:, None], runs(a_l, H)] - (y[np.arange(H)[:, None], runs(b_l, H)])
    z = f64(gn) * (d * (-1.0 * (f64(rest) / (np.abs(d) + 0.25)) + 1))
    return mxq(f64(w2), 0, "e4m3").T @ mxq(z, 0, "e4m3")

@@ -1,0 +1,156 @@
+from contextlib import ExitStack
+
+import concourse.mybir as mybir
+
+K, T, S, V, N, H = 512, 2048, 512, 256, 512, 512
+FLOPS = 2 * K * H * S + 2 * H * N * V
+
+F32 = mybir.dt.float32
+BF16 = mybir.dt.bfloat16
+I32 = mybir.dt.int32
+U32 = mybir.dt.uint32
+U16 = mybir.dt.uint16
+U8 = mybir.dt.uint8
+FP8X4 = mybir.dt.float8_e4m3fn_x4
+ACT = mybir.ActivationFunctionType
+ALU = mybir.AluOpType
+
+P = 128
+PACK = 4
+HALF_M = 64
+HALF_V = V // 2
+
+
+def tile_picked_restlen_none_p_kernel(tc, x_words, x_scales, w1, rest, gn, w2, offs, a_l, b_l, out):
+    nc = tc.nc
+    with ExitStack() as ctx:
+        keep = ctx.enter_context(tc.tile_pool(name="keep", bufs=1))
+        psum = ctx.enter_context(tc.psum_pool(name="psum", bufs=1))
+
+        def sb(name, shape, dtype):
+            return keep.tile(shape, dtype, name=name, align_bytes=64)
+
+        offs_sb = sb("offs_sb", [P, S // 16], U16)
+        a_sb = sb("a_sb", [P, V // 16], U16)
+        b_sb = sb("b_sb", [P, V // 16], U16)
+        xw_all = sb("xw_all", [P, T], I32)
+        xs_all = sb("xs_all", [P, T], U8)
+        w1_raw = [sb(f"w1_raw{h}", [P, PACK, H // 2], F32) for h in range(2)]
+        w2_raw = sb("w2_raw", [P, PACK, N], F32)
+        rest_sb = sb("rest_sb", [P, PACK, V], F32)
+        gn_sb = sb("gn_sb", [P, PACK], F32)
+
+        w1_rows = w1.rearrange("(p j) c -> p j c", j=PACK)
+        nc.vector.memset(xs_all[:].bitcast(I32), 0)
+        nc.sync.dma_start(offs_sb[:], offs)
+        for h in range(2):
+            nc.sync.dma_start(w1_raw[h][:], w1_rows[:, :, h * (H // 2) : (h + 1) * (H // 2)])
+        for q in range(4):
+            nc.sync.dma_start(xs_all[32 * q : 32 * q + 4, :].bitcast(I32), x_scales[0, 4 * q : 4 * q + 4, :].bitcast(I32))
+        nc.sync.dma_start(xw_all[:], x_words[0].rearrange("p c r -> p (c r)").bitcast(I32))
+        nc.sync.dma_start(b_sb[:], b_l)
+        nc.sync.dma_start(w2_raw[:], w2.rearrange("(p j) c -> p j c", j=PACK))
+        nc.sync.dma_start(a_sb[:], a_l)
+        nc.sync.dma_start(rest_sb[:], rest.rearrange("(p j) c -> p j c", j=PACK))
+        nc.sync.dma_start(gn_sb[:], gn.rearrange("(p j) o -> p (j o)", j=PACK))
+
+        xw = sb("xw", [P, S], U32)
+        xs = sb("xs", [P, S], U8)
+        w1_words = sb("w1_words", [P, H], U32)
+        w1_scales = sb("w1_scales", [P, H], U8)
+        w1_bf = sb("w1_bf", [P, PACK, P, PACK], BF16)
+
+        def deal(h):
+            return (
+                w1_bf[:, :, h * HALF_M : (h + 1) * HALF_M, :].rearrange("p t m j -> p m j t"),
+                w1_raw[h][:].rearrange("p j (m t) -> p m j t", t=PACK),
+            )
+
+        nc.vector.tensor_copy(*deal(0))
+        nc.vector.tensor_copy(xs[:], xs_all[:].indirect(offs_sb[:]))
+        nc.scalar.copy(*deal(1))
+        for g in range(2):
+            nc.vector.quantize_mx(
+                out=w1_words[:, g * 256 : (g + 1) * 256].bitcast(FP8X4),
+                scales=w1_scales[:, g * 256 : (g + 1) * 256],
+                in_=w1_bf[:, 2 * g : 2 * g + 2].rearrange("p t m j -> p (t m j)"),
+            )
+
+        HS = S // 2
+        for g in range(2):
+            nc.vector.tensor_copy(xw[:, g * HS : (g + 1) * HS], xw_all[:].bitcast(U32).indirect(offs_sb[:, g * HS // 16 : (g + 1) * HS // 16]))
+
+        y = [sb(f"y{t}", [P, S], F32) for t in range(PACK)]
+        y_acc = {}
+        for t, g in ((0, 0), (1, 0), (0, 1), (1, 1), (2, 0), (2, 1), (3, 0), (3, 1)):
+            js = slice(g * HS, (g + 1) * HS)
+            mc = slice(t * P, (t + 1) * P)
+            y_acc[t, g] = psum.tile([P, HS], F32, name=f"y_acc{t}{g}", tag=f"bank{t}{g}")
+            nc.tensor.matmul_mx(out=y_acc[t, g][:], lhsT=w1_words[:, mc].bitcast(FP8X4), lhsT_scale=w1_scales[:, mc], rhs=xw[:, js].bitcast(FP8X4), rhs_scale=xs[:, js], start=True, stop=True)
+        for t in range(PACK):
+            for g in range(2):
+                nc.scalar.copy(y[t][:, g * HS : (g + 1) * HS], y_acc[t, g][:])
+
+        w2_bf = sb("w2_bf", [P, N * PACK], BF16)
+        w2_words = sb("w2_words", [P, N], U32)
+        w2_scales = sb("w2_scales", [P, N], U8)
+        nd = [sb(f"nd{h}", [P, PACK, HALF_V], F32) for h in range(2)]
+        ya = [sb(f"ya{h}", [P, PACK, HALF_V], F32) for h in range(2)]
+        mag = [sb(f"mag{h}", [P, PACK, HALF_V], F32) for h in range(2)]
+        sq = [sb(f"sq{h}", [P, PACK, HALF_V], F32) for h in range(2)]
+        inv = [sb(f"inv{h}", [P, PACK, HALF_V], F32) for h in range(2)]
+        slack = [sb(f"slack{h}", [P, PACK, HALF_V], F32) for h in range(2)]
+        num = [sb(f"num{h}", [P, PACK, HALF_V], F32) for h in range(2)]
+        z_bf = [sb(f"z_bf{h}", [P, HALF_V * PACK], BF16) for h in range(2)]
+        z_words = [sb(f"z_words{h}", [P, HALF_V], U32) for h in range(2)]
+        z_scales = [sb(f"z_scales{h}", [P, HALF_V], U8) for h in range(2)]
+        out_rows = out.rearrange("(u p) v -> p u v", p=P)
+
+        for h in range(2):
+            lc = slice(h * HALF_V // 16, (h + 1) * HALF_V // 16)
+            for t in range(PACK):
+                nc.scalar.activation(ya[h][:, t, :], y[t][:].indirect(b_sb[:, lc]), ACT.Copy)
+                nc.vector.tensor_tensor(nd[h][:, t, :], y[t][:].indirect(a_sb[:, lc]), ya[h][:, t, :], ALU.subtract)
+
+        for h in range(2):
+            vs = slice(h * HALF_V, (h + 1) * HALF_V)
+            pairs = (slice(0, 2), slice(2, 4))
+            for ts in pairs:
+                nc.scalar.activation(mag[h][:, ts, :], nd[h][:, ts, :], ACT.Abs)
+            for ts in pairs:
+                nc.scalar.activation(sq[h][:, ts, :], mag[h][:, ts, :], ACT.Square, bias=0.25)
+            for ts in pairs:
+                nc.scalar.activation(inv[h][:, ts, :], sq[h][:, ts, :], ACT.Abs_reciprocal_sqrt)
+            for ts in pairs:
+                nc.vector.scalar_tensor_tensor(slack[h][:, ts, :], mag[h][:, ts, :], 0.25, rest_sb[:, ts, vs], ALU.add, ALU.subtract)
+            for t in range(PACK):
+                nc.vector.scalar_tensor_tensor(num[h][:, t, :], nd[h][:, t, :], gn_sb[:, t : t + 1], slack[h][:, t, :], ALU.mult, ALU.mult)
+            nc.vector.tensor_tensor(
+                z_bf[h][:].rearrange("p (c i t) -> p c t i", i=4, t=PACK),
+                num[h][:].rearrange("p t (c i) -> p c t i", i=4),
+                inv[h][:].rearrange("p t (c i) -> p c t i", i=4),
+                ALU.mult,
+            )
+            nc.vector.quantize_mx(out=z_words[h][:].bitcast(FP8X4), scales=z_scales[h][:], in_=z_bf[h][:])
+
+        for u in range(4):
+            nc.vector.tensor_copy(
+                w2_bf[:, u * P * PACK : (u + 1) * P * PACK].rearrange("p (c i j) -> p c j i", i=4, j=PACK),
+                w2_raw[:, :, u * P : (u + 1) * P].rearrange("p j (c i) -> p c j i", i=4),
+            )
+        for g in range(2):
+            nc.vector.quantize_mx(out=w2_words[:, g * 256 : (g + 1) * 256].bitcast(FP8X4), scales=w2_scales[:, g * 256 : (g + 1) * 256], in_=w2_bf[:, g * 1024 : (g + 1) * 1024])
+
+        for h in range(2):
+            vs = slice(h * HALF_V, (h + 1) * HALF_V)
+            for g in range(2):
+                acc = psum.tile([P, 2, HALF_V], F32, name=f"out_acc{h}{g}", tag=f"bank{h}{g}")
+                for e in range(2):
+                    mc = slice((2 * g + e) * P, (2 * g + e + 1) * P)
+                    nc.tensor.matmul_mx(out=acc[:, e, :], lhsT=w2_words[:, mc].bitcast(FP8X4), lhsT_scale=w2_scales[:, mc], rhs=z_words[h][:].bitcast(FP8X4), rhs_scale=z_scales[h][:], start=True, stop=True)
+                res = sb(f"res{h}{g}", [P, 2, HALF_V], F32)
+                if g == 0 or h == 0:
+                    nc.scalar.copy(res[:], acc[:])
+                else:
+                    nc.vector.tensor_copy(res[:], acc[:])
+                nc.sync.dma_start(out_rows[:, 2 * g : 2 * g + 2, vs], res[:])

@@ -40,6 +40,10 @@ def tile_picked_restlen_none_p_kernel(tc, x_words, x_scales, w1, rest, gn, w2, o
         rest_sb = sb("rest_sb", [P, PACK, V], F32)
         gn_sb = sb("gn_sb", [P, PACK], F32)
 
+        warm_in = sb("warm_in", [P, 1], F32)
+        warm_out = sb("warm_out", [P, 1], F32)
+        nc.vector.memset(warm_in[:], 1.0)
+        nc.scalar.activation(warm_out[:], warm_in[:], ACT.Abs_reciprocal_sqrt)
         w1_rows = w1.rearrange("(p j) c -> p j c", j=PACK)
         nc.vector.memset(xs_all[:].bitcast(I32), 0)
         nc.sync.dma_start(offs_sb[:], offs)

@@ -27,22 +27,22 @@ def tile_picked_restlen_none_p_kernel(tc, x_words, x_scales, w1, rest, gn, w2, o
         keep = ctx.enter_context(tc.tile_pool(name="keep", bufs=1))
         psum = ctx.enter_context(tc.psum_pool(name="psum", bufs=1))
 
-        def sb(name, shape, dtype):
-            return keep.tile(shape, dtype, name=name, align_bytes=64)
+        def sb(name, shape, dtype, tag=None):
+            return keep.tile(shape, dtype, name=name, tag=tag or name, align_bytes=64)
 
         offs_sb = sb("offs_sb", [P, S // 16], U16)
         a_sb = sb("a_sb", [P, V // 16], U16)
         b_sb = sb("b_sb", [P, V // 16], U16)
         xw_all = sb("xw_all", [P, T], I32)
-        xs_all = sb("xs_all", [P, T], U8)
+        xs_all = sb("xs_all", [P, T], U8, "scale_bytes")
         w1_raw = [sb(f"w1_raw{h}", [P, PACK, H // 2], F32) for h in range(2)]
-        w2_raw = sb("w2_raw", [P, PACK, N], F32)
+        w2_raw = [sb(f"w2_raw{g}", [P, PACK, N // 2], F32, f"w2_half{g}") for g in range(2)]
         rest_sb = sb("rest_sb", [P, PACK, V], F32)
         gn_sb = sb("gn_sb", [P, PACK], F32)
 
         warm_in = sb("warm_in", [P, 1], F32)
         warm_out = sb("warm_out", [P, 1], F32)
-        nc.vector.memset(warm_in[:], 1.0)
+        nc.gpsimd.memset(warm_in[:], 1.0)
         nc.scalar.activation(warm_out[:], warm_in[:], ACT.Abs_reciprocal_sqrt)
         w1_rows = w1.rearrange("(p j) c -> p j c", j=PACK)
         nc.vector.memset(xs_all[:].bitcast(I32), 0)
@@ -53,26 +53,28 @@ def tile_picked_restlen_none_p_kernel(tc, x_words, x_scales, w1, rest, gn, w2, o
             nc.sync.dma_start(xs_all[32 * q : 32 * q + 4, :].bitcast(I32), x_scales[0, 4 * q : 4 * q + 4, :].bitcast(I32))
         nc.sync.dma_start(xw_all[:], x_words[0].rearrange("p c r -> p (c r)").bitcast(I32))
         nc.sync.dma_start(b_sb[:], b_l)
-        nc.sync.dma_start(w2_raw[:], w2.rearrange("(p j) c -> p j c", j=PACK))
+        w2_rows = w2.rearrange("(p j) c -> p j c", j=PACK)
+        nc.sync.dma_start(w2_raw[0][:], w2_rows[:, :, 0 : N // 2])
         nc.sync.dma_start(a_sb[:], a_l)
+        nc.sync.dma_start(w2_raw[1][:], w2_rows[:, :, N // 2 : N])
         nc.sync.dma_start(rest_sb[:], rest.rearrange("(p j) c -> p j c", j=PACK))
         nc.sync.dma_start(gn_sb[:], gn.rearrange("(p j) o -> p (j o)", j=PACK))
 
         xw = sb("xw", [P, S], U32)
         xs = sb("xs", [P, S], U8)
         w1_words = sb("w1_words", [P, H], U32)
-        w1_scales = sb("w1_scales", [P, H], U8)
+        w1_scales = sb("w1_scales", [P, H], U8, "scale_bytes")
         w1_bf = sb("w1_bf", [P, PACK, P, PACK], BF16)
 
-        def deal(h):
+        def deal(h, m0, m1):
             return (
-                w1_bf[:, :, h * HALF_M : (h + 1) * HALF_M, :].rearrange("p t m j -> p m j t"),
-                w1_raw[h][:].rearrange("p j (m t) -> p m j t", t=PACK),
+                w1_bf[:, :, h * HALF_M + m0 : h * HALF_M + m1, :].rearrange("p t m j -> p m j t"),
+                w1_raw[h][:, :, m0 * PACK : m1 * PACK].rearrange("p j (m t) -> p m j t", t=PACK),
             )
 
-        nc.vector.tensor_copy(*deal(0))
+        nc.vector.tensor_copy(*deal(0, 0, HALF_M))
+        nc.scalar.copy(*deal(1, 0, HALF_M))
         nc.vector.tensor_copy(xs[:], xs_all[:].indirect(offs_sb[:]))
-        nc.scalar.copy(*deal(1))
         for g in range(2):
             nc.vector.quantize_mx(
                 out=w1_words[:, g * 256 : (g + 1) * 256].bitcast(FP8X4),
@@ -84,7 +86,17 @@ def tile_picked_restlen_none_p_kernel(tc, x_words, x_scales, w1, rest, gn, w2, o
         for g in range(2):
             nc.vector.tensor_copy(xw[:, g * HS : (g + 1) * HS], xw_all[:].bitcast(U32).indirect(offs_sb[:, g * HS // 16 : (g + 1) * HS // 16]))
 
-        y = [sb(f"y{t}", [P, S], F32) for t in range(PACK)]
+        w2_bf = sb("w2_bf", [P, N * PACK], BF16, "w2_rounded")
+        w2_words = sb("w2_words", [P, N], U32)
+        w2_scales = sb("w2_scales", [P, N], U8)
+        for g in range(2):
+            nc.vector.tensor_copy(
+                w2_bf[:, g * 1024 : (g + 1) * 1024].rearrange("p (c i j) -> p c j i", i=4, j=PACK),
+                w2_raw[g][:].rearrange("p j (c i) -> p c j i", i=4),
+            )
+            nc.vector.quantize_mx(out=w2_words[:, g * 256 : (g + 1) * 256].bitcast(FP8X4), scales=w2_scales[:, g * 256 : (g + 1) * 256], in_=w2_bf[:, g * 1024 : (g + 1) * 1024])
+
+        y = [sb(f"y{t}", [P, S], F32, "w2_half1" if t == PACK - 1 else None) for t in range(PACK)]
         y_acc = {}
         for t, g in ((0, 0), (1, 0), (0, 1), (1, 1), (2, 0), (2, 1), (3, 0), (3, 1)):
             js = slice(g * HS, (g + 1) * HS)
@@ -93,42 +105,43 @@ def tile_picked_restlen_none_p_kernel(tc, x_words, x_scales, w1, rest, gn, w2, o
             nc.tensor.matmul_mx(out=y_acc[t, g][:], lhsT=w1_words[:, mc].bitcast(FP8X4), lhsT_scale=w1_scales[:, mc], rhs=xw[:, js].bitcast(FP8X4), rhs_scale=xs[:, js], start=True, stop=True)
         for t in range(PACK):
             for g in range(2):
-                nc.scalar.copy(y[t][:, g * HS : (g + 1) * HS], y_acc[t, g][:])
+                if t == PACK - 1:
+                    nc.vector.tensor_copy(y[t][:, g * HS : (g + 1) * HS], y_acc[t, g][:])
+                else:
+                    nc.scalar.copy(y[t][:, g * HS : (g + 1) * HS], y_acc[t, g][:])
 
-        w2_bf = sb("w2_bf", [P, N * PACK], BF16)
-        w2_words = sb("w2_words", [P, N], U32)
-        w2_scales = sb("w2_scales", [P, N], U8)
-        nd = [sb(f"nd{h}", [P, PACK, HALF_V], F32) for h in range(2)]
-        ya = [sb(f"ya{h}", [P, PACK, HALF_V], F32) for h in range(2)]
-        mag = [sb(f"mag{h}", [P, PACK, HALF_V], F32) for h in range(2)]
+        ya = sb("ya", [P, PACK, V], F32)
+        mag = sb("mag", [P, PACK, V], F32)
+        slack = sb("slack", [P, PACK, V], F32)
         sq = [sb(f"sq{h}", [P, PACK, HALF_V], F32) for h in range(2)]
         inv = [sb(f"inv{h}", [P, PACK, HALF_V], F32) for h in range(2)]
-        slack = [sb(f"slack{h}", [P, PACK, HALF_V], F32) for h in range(2)]
         num = [sb(f"num{h}", [P, PACK, HALF_V], F32) for h in range(2)]
         z_bf = [sb(f"z_bf{h}", [P, HALF_V * PACK], BF16) for h in range(2)]
         z_words = [sb(f"z_words{h}", [P, HALF_V], U32) for h in range(2)]
         z_scales = [sb(f"z_scales{h}", [P, HALF_V], U8) for h in range(2)]
         out_rows = out.rearrange("(u p) v -> p u v", p=P)
 
-        for h in range(2):
-            lc = slice(h * HALF_V // 16, (h + 1) * HALF_V // 16)
-            for t in range(PACK):
-                nc.scalar.activation(ya[h][:, t, :], y[t][:].indirect(b_sb[:, lc]), ACT.Copy)
-                nc.vector.tensor_tensor(nd[h][:, t, :], y[t][:].indirect(a_sb[:, lc]), ya[h][:, t, :], ALU.subtract)
+        nd = sb("nd", [P, PACK, V], F32, "w2_rounded")
+        for t in range(PACK):
+            nc.scalar.activation(ya[:, t, :], y[t][:].indirect(b_sb[:]), ACT.Copy)
+            nc.vector.tensor_tensor(nd[:, t, :], y[t][:].indirect(a_sb[:]), ya[:, t, :], ALU.subtract)
+        for t in range(PACK):
+            nc.scalar.activation(mag[:, t, :], nd[:, t, :], ACT.Abs)
 
+        pairs = (slice(0, 2), slice(2, 4))
         for h in range(2):
             vs = slice(h * HALF_V, (h + 1) * HALF_V)
-            pairs = (slice(0, 2), slice(2, 4))
             for ts in pairs:
-                nc.scalar.activation(mag[h][:, ts, :], nd[h][:, ts, :], ACT.Abs)
-            for ts in pairs:
-                nc.scalar.activation(sq[h][:, ts, :], mag[h][:, ts, :], ACT.Square, bias=0.25)
+                nc.scalar.activation(sq[h][:, ts, :], mag[:, ts, vs], ACT.Square, bias=0.25)
             for ts in pairs:
                 nc.scalar.activation(inv[h][:, ts, :], sq[h][:, ts, :], ACT.Abs_reciprocal_sqrt)
-            for ts in pairs:
-                nc.vector.scalar_tensor_tensor(slack[h][:, ts, :], mag[h][:, ts, :], 0.25, rest_sb[:, ts, vs], ALU.add, ALU.subtract)
+        for h in range(2):
+            vs = slice(h * HALF_V, (h + 1) * HALF_V)
             for t in range(PACK):
-                nc.vector.scalar_tensor_tensor(num[h][:, t, :], nd[h][:, t, :], gn_sb[:, t : t + 1], slack[h][:, t, :], ALU.mult, ALU.mult)
+                if h == 0 and t % 2 == 0:
+                    ts = pairs[t // 2]
+                    nc.vector.scalar_tensor_tensor(slack[:, ts, :], mag[:, ts, :], 0.25, rest_sb[:, ts, :], ALU.add, ALU.subtract)
+                nc.vector.scalar_tensor_tensor(num[h][:, t, :], nd[:, t, vs], gn_sb[:, t : t + 1], slack[:, t, vs], ALU.mult, ALU.mult)
             nc.vector.tensor_tensor(
                 z_bf[h][:].rearrange("p (c i t) -> p c t i", i=4, t=PACK),
                 num[h][:].rearrange("p t (c i) -> p c t i", i=4),
@@ -137,24 +150,16 @@ def tile_picked_restlen_none_p_kernel(tc, x_words, x_scales, w1, rest, gn, w2, o
             )
             nc.vector.quantize_mx(out=z_words[h][:].bitcast(FP8X4), scales=z_scales[h][:], in_=z_bf[h][:])
 
-        for u in range(4):
-            nc.vector.tensor_copy(
-                w2_bf[:, u * P * PACK : (u + 1) * P * PACK].rearrange("p (c i j) -> p c j i", i=4, j=PACK),
-                w2_raw[:, :, u * P : (u + 1) * P].rearrange("p j (c i) -> p c j i", i=4),
-            )
-        for g in range(2):
-            nc.vector.quantize_mx(out=w2_words[:, g * 256 : (g + 1) * 256].bitcast(FP8X4), scales=w2_scales[:, g * 256 : (g + 1) * 256], in_=w2_bf[:, g * 1024 : (g + 1) * 1024])
-
         for h in range(2):
             vs = slice(h * HALF_V, (h + 1) * HALF_V)
             for g in range(2):
-                acc = psum.tile([P, 2, HALF_V], F32, name=f"out_acc{h}{g}", tag=f"bank{h}{g}")
+                res = sb(f"res{h}{g}", [P, 2, HALF_V], F32)
                 for e in range(2):
                     mc = slice((2 * g + e) * P, (2 * g + e + 1) * P)
-                    nc.tensor.matmul_mx(out=acc[:, e, :], lhsT=w2_words[:, mc].bitcast(FP8X4), lhsT_scale=w2_scales[:, mc], rhs=z_words[h][:].bitcast(FP8X4), rhs_scale=z_scales[h][:], start=True, stop=True)
-                res = sb(f"res{h}{g}", [P, 2, HALF_V], F32)
-                if g == 0 or h == 0:
-                    nc.scalar.copy(res[:], acc[:])
-                else:
-                    nc.vector.tensor_copy(res[:], acc[:])
+                    acc = psum.tile([P, HALF_V], F32, name=f"out_acc{h}{g}{e}", tag=f"bank{2 * h + g}{e}")
+                    nc.tensor.matmul_mx(out=acc[:], lhsT=w2_words[:, mc].bitcast(FP8X4), lhsT_scale=w2_scales[:, mc], rhs=z_words[h][:].bitcast(FP8X4), rhs_scale=z_scales[h][:], start=True, stop=True)
+                    if h == 0 or e == 0:
+                        nc.scalar.copy(res[:, e, :], acc[:])
+                    else:
+                        nc.vector.tensor_copy(res[:, e, :], acc[:])
                 nc.sync.dma_start(out_rows[:, 2 * g : 2 * g + 2, vs], res[:])

@@ -46,11 +46,11 @@ def tile_picked_restlen_none_p_kernel(tc, x_words, x_scales, w1, rest, gn, w2, o
         nc.scalar.activation(warm_out[:], warm_in[:], ACT.Abs_reciprocal_sqrt)
         w1_rows = w1.rearrange("(p j) c -> p j c", j=PACK)
         nc.vector.memset(xs_all[:].bitcast(I32), 0)
+        nc.sync.dma_start(w1_raw[0][:], w1_rows[:, :, 0 : H // 2])
         nc.sync.dma_start(offs_sb[:], offs)
-        for h in range(2):
-            nc.sync.dma_start(w1_raw[h][:], w1_rows[:, :, h * (H // 2) : (h + 1) * (H // 2)])
-        for q in range(4):
-            nc.sync.dma_start(xs_all[32 * q : 32 * q + 4, :].bitcast(I32), x_scales[0, 4 * q : 4 * q + 4, :].bitcast(I32))
+        nc.sync.dma_start(w1_raw[1][:], w1_rows[:, :, H // 2 : H])
+        for r in range(4):
+            nc.sync.dma_start(xs_all[r:P:32, :].bitcast(I32), x_scales[0, r:16:4, :].bitcast(I32))
         nc.sync.dma_start(xw_all[:], x_words[0].rearrange("p c r -> p (c r)").bitcast(I32))
         nc.sync.dma_start(b_sb[:], b_l)
         w2_rows = w2.rearrange("(p j) c -> p j c", j=PACK)
@@ -82,9 +82,8 @@ def tile_picked_restlen_none_p_kernel(tc, x_words, x_scales, w1, rest, gn, w2, o
                 in_=w1_bf[:, 2 * g : 2 * g + 2].rearrange("p t m j -> p (t m j)"),
             )
 
-        HS = S // 2
-        for g in range(2):
-            nc.vector.tensor_copy(xw[:, g * HS : (g + 1) * HS], xw_all[:].bitcast(U32).indirect(offs_sb[:, g * HS // 16 : (g + 1) * HS // 16]))
+        for j0, j1 in ((0, 128), (128, 256), (256, 512)):
+            nc.vector.tensor_copy(xw[:, j0:j1], xw_all[:].bitcast(U32).indirect(offs_sb[:, j0 // 16 : j1 // 16]))
 
         w2_bf = sb("w2_bf", [P, N * PACK], BF16, "w2_rounded")
         w2_words = sb("w2_words", [P, N], U32)
@@ -97,18 +96,15 @@ def tile_picked_restlen_none_p_kernel(tc, x_words, x_scales, w1, rest, gn, w2, o
             nc.vector.quantize_mx(out=w2_words[:, g * 256 : (g + 1) * 256].bitcast(FP8X4), scales=w2_scales[:, g * 256 : (g + 1) * 256], in_=w2_bf[:, g * 1024 : (g + 1) * 1024])
 
         y = [sb(f"y{t}", [P, S], F32, "w2_half1" if t == PACK - 1 else None) for t in range(PACK)]
-        y_acc = {}
-        for t, g in ((0, 0), (1, 0), (0, 1), (1, 1), (2, 0), (2, 1), (3, 0), (3, 1)):
-            js = slice(g * HS, (g + 1) * HS)
+        pieces = ((0, 0, 128), (1, 0, 128), (0, 128, 256), (1, 128, 256), (2, 0, 256), (0, 256, 512), (1, 256, 512), (2, 256, 512), (3, 0, 256), (3, 256, 512))
+        for n, (t, j0, j1) in enumerate(pieces):
             mc = slice(t * P, (t + 1) * P)
-            y_acc[t, g] = psum.tile([P, HS], F32, name=f"y_acc{t}{g}", tag=f"bank{t}{g}")
-            nc.tensor.matmul_mx(out=y_acc[t, g][:], lhsT=w1_words[:, mc].bitcast(FP8X4), lhsT_scale=w1_scales[:, mc], rhs=xw[:, js].bitcast(FP8X4), rhs_scale=xs[:, js], start=True, stop=True)
-        for t in range(PACK):
-            for g in range(2):
-                if t == PACK - 1:
-                    nc.vector.tensor_copy(y[t][:, g * HS : (g + 1) * HS], y_acc[t, g][:])
-                else:
-                    nc.scalar.copy(y[t][:, g * HS : (g + 1) * HS], y_acc[t, g][:])
+            acc = psum.tile([P, j1 - j0], F32, name=f"y_acc{n}", tag=f"bank{n % 8}")
+            nc.tensor.matmul_mx(out=acc[:], lhsT=w1_words[:, mc].bitcast(FP8X4), lhsT_scale=w1_scales[:, mc], rhs=xw[:, j0:j1].bitcast(FP8X4), rhs_scale=xs[:, j0:j1], start=True, stop=True)
+            if t == PACK - 1:
+                nc.vector.tensor_copy(y[t][:, j0:j1], acc[:])
+            else:
+                nc.scalar.copy(y[t][:, j0:j1], acc[:])
 
         ya = sb("ya", [P, PACK, V], F32)
         mag = sb("mag", [P, PACK, V], F32)
@@ -156,7 +152,7 @@ def tile_picked_restlen_none_p_kernel(tc, x_words, x_scales, w1, rest, gn, w2, o
                 res = sb(f"res{h}{g}", [P, 2, HALF_V], F32)
                 for e in range(2):
                     mc = slice((2 * g + e) * P, (2 * g + e + 1) * P)
-                    acc = psum.tile([P, HALF_V], F32, name=f"out_acc{h}{g}{e}", tag=f"bank{2 * h + g}{e}")
+                    acc = psum.tile([P, HALF_V], F32, name=f"out_acc{h}{g}{e}", tag=f"bank{(2 + 4 * h + 2 * g + e) % 8}")
                     nc.tensor.matmul_mx(out=acc[:], lhsT=w2_words[:, mc].bitcast(FP8X4), lhsT_scale=w2_scales[:, mc], rhs=z_words[h][:].bitcast(FP8X4), rhs_scale=z_scales[h][:], start=True, stop=True)
                     if h == 0 or e == 0:
                         nc.scalar.copy(res[:, e, :], acc[:])

from contextlib import ExitStack

import concourse.mybir as mybir

K, T, S, V, N, H = 512, 2048, 512, 256, 512, 512
FLOPS = 2 * K * H * S + 2 * H * N * V

F32 = mybir.dt.float32
BF16 = mybir.dt.bfloat16
I32 = mybir.dt.int32
U32 = mybir.dt.uint32
U16 = mybir.dt.uint16
U8 = mybir.dt.uint8
FP8X4 = mybir.dt.float8_e4m3fn_x4
ACT = mybir.ActivationFunctionType
ALU = mybir.AluOpType

P = 128
PACK = 4
HALF_M = 64
HALF_V = V // 2


def tile_picked_restlen_none_p_kernel(tc, x_words, x_scales, w1, rest, gn, w2, offs, a_l, b_l, out):
    nc = tc.nc
    with ExitStack() as ctx:
        keep = ctx.enter_context(tc.tile_pool(name="keep", bufs=1))
        psum = ctx.enter_context(tc.psum_pool(name="psum", bufs=1))

        def sb(name, shape, dtype, tag=None):
            return keep.tile(shape, dtype, name=name, tag=tag or name, align_bytes=64)

        offs_sb = sb("offs_sb", [P, S // 16], U16)
        a_sb = sb("a_sb", [P, V // 16], U16)
        b_sb = sb("b_sb", [P, V // 16], U16)
        xw_all = sb("xw_all", [P, T], I32)
        xs_all = sb("xs_all", [P, T], U8, "scale_bytes")
        w1_raw = [sb(f"w1_raw{h}", [P, PACK, H // 2], F32) for h in range(2)]
        w2_raw = [sb(f"w2_raw{g}", [P, PACK, N // 2], F32, f"w2_half{g}") for g in range(2)]
        rest_sb = sb("rest_sb", [P, PACK, V], F32)
        gn_sb = sb("gn_sb", [P, PACK], F32)

        warm_in = sb("warm_in", [P, 1], F32)
        warm_out = sb("warm_out", [P, 1], F32)
        nc.gpsimd.memset(warm_in[:], 1.0)
        nc.scalar.activation(warm_out[:], warm_in[:], ACT.Abs_reciprocal_sqrt)
        w1_rows = w1.rearrange("(p j) c -> p j c", j=PACK)
        nc.vector.memset(xs_all[:].bitcast(I32), 0)
        nc.sync.dma_start(w1_raw[0][:], w1_rows[:, :, 0 : H // 2])
        nc.sync.dma_start(offs_sb[:], offs)
        nc.sync.dma_start(w1_raw[1][:], w1_rows[:, :, H // 2 : H])
        for r in range(4):
            nc.sync.dma_start(xs_all[r:P:32, :].bitcast(I32), x_scales[0, r:16:4, :].bitcast(I32))
        nc.sync.dma_start(xw_all[:], x_words[0].rearrange("p c r -> p (c r)").bitcast(I32))
        nc.sync.dma_start(b_sb[:], b_l)
        w2_rows = w2.rearrange("(p j) c -> p j c", j=PACK)
        nc.sync.dma_start(w2_raw[0][:], w2_rows[:, :, 0 : N // 2])
        nc.sync.dma_start(a_sb[:], a_l)
        nc.sync.dma_start(w2_raw[1][:], w2_rows[:, :, N // 2 : N])
        nc.sync.dma_start(rest_sb[:], rest.rearrange("(p j) c -> p j c", j=PACK))
        nc.sync.dma_start(gn_sb[:], gn.rearrange("(p j) o -> p (j o)", j=PACK))

        xw = sb("xw", [P, S], U32)
        xs = sb("xs", [P, S], U8)
        w1_words = sb("w1_words", [P, H], U32)
        w1_scales = sb("w1_scales", [P, H], U8, "scale_bytes")
        w1_bf = sb("w1_bf", [P, PACK, P, PACK], BF16)

        def deal(h, m0, m1):
            return (
                w1_bf[:, :, h * HALF_M + m0 : h * HALF_M + m1, :].rearrange("p t m j -> p m j t"),
                w1_raw[h][:, :, m0 * PACK : m1 * PACK].rearrange("p j (m t) -> p m j t", t=PACK),
            )

        nc.vector.tensor_copy(*deal(0, 0, HALF_M))
        nc.scalar.copy(*deal(1, 0, HALF_M))
        nc.vector.tensor_copy(xs[:], xs_all[:].indirect(offs_sb[:]))
        for g in range(2):
            nc.vector.quantize_mx(
                out=w1_words[:, g * 256 : (g + 1) * 256].bitcast(FP8X4),
                scales=w1_scales[:, g * 256 : (g + 1) * 256],
                in_=w1_bf[:, 2 * g : 2 * g + 2].rearrange("p t m j -> p (t m j)"),
            )

        for j0, j1 in ((0, 128), (128, 256), (256, 512)):
            nc.vector.tensor_copy(xw[:, j0:j1], xw_all[:].bitcast(U32).indirect(offs_sb[:, j0 // 16 : j1 // 16]))

        w2_bf = sb("w2_bf", [P, N * PACK], BF16, "w2_rounded")
        w2_words = sb("w2_words", [P, N], U32)
        w2_scales = sb("w2_scales", [P, N], U8)
        for g in range(2):
            nc.vector.tensor_copy(
                w2_bf[:, g * 1024 : (g + 1) * 1024].rearrange("p (c i j) -> p c j i", i=4, j=PACK),
                w2_raw[g][:].rearrange("p j (c i) -> p c j i", i=4),
            )
            nc.vector.quantize_mx(out=w2_words[:, g * 256 : (g + 1) * 256].bitcast(FP8X4), scales=w2_scales[:, g * 256 : (g + 1) * 256], in_=w2_bf[:, g * 1024 : (g + 1) * 1024])

        y = [sb(f"y{t}", [P, S], F32, "w2_half1" if t == PACK - 1 else None) for t in range(PACK)]
        pieces = ((0, 0, 128), (1, 0, 128), (0, 128, 256), (1, 128, 256), (2, 0, 256), (0, 256, 512), (1, 256, 512), (2, 256, 512), (3, 0, 256), (3, 256, 512))
        for n, (t, j0, j1) in enumerate(pieces):
            mc = slice(t * P, (t + 1) * P)
            acc = psum.tile([P, j1 - j0], F32, name=f"y_acc{n}", tag=f"bank{n % 8}")
            nc.tensor.matmul_mx(out=acc[:], lhsT=w1_words[:, mc].bitcast(FP8X4), lhsT_scale=w1_scales[:, mc], rhs=xw[:, j0:j1].bitcast(FP8X4), rhs_scale=xs[:, j0:j1], start=True, stop=True)
            if t == PACK - 1:
                nc.vector.tensor_copy(y[t][:, j0:j1], acc[:])
            else:
                nc.scalar.copy(y[t][:, j0:j1], acc[:])

        ya = sb("ya", [P, PACK, V], F32)
        mag = sb("mag", [P, PACK, V], F32)
        slack = sb("slack", [P, PACK, V], F32)
        sq = [sb(f"sq{h}", [P, PACK, HALF_V], F32) for h in range(2)]
        inv = [sb(f"inv{h}", [P, PACK, HALF_V], F32) for h in range(2)]
        num = [sb(f"num{h}", [P, PACK, HALF_V], F32) for h in range(2)]
        z_bf = [sb(f"z_bf{h}", [P, HALF_V * PACK], BF16) for h in range(2)]
        z_words = [sb(f"z_words{h}", [P, HALF_V], U32) for h in range(2)]
        z_scales = [sb(f"z_scales{h}", [P, HALF_V], U8) for h in range(2)]
        out_rows = out.rearrange("(u p) v -> p u v", p=P)

        nd = sb("nd", [P, PACK, V], F32, "w2_rounded")
        for t in range(PACK):
            nc.scalar.activation(ya[:, t, :], y[t][:].indirect(b_sb[:]), ACT.Copy)
            nc.vector.tensor_tensor(nd[:, t, :], y[t][:].indirect(a_sb[:]), ya[:, t, :], ALU.subtract)
        for t in range(PACK):
            nc.scalar.activation(mag[:, t, :], nd[:, t, :], ACT.Abs)

        pairs = (slice(0, 2), slice(2, 4))
        for h in range(2):
            vs = slice(h * HALF_V, (h + 1) * HALF_V)
            for ts in pairs:
                nc.scalar.activation(sq[h][:, ts, :], mag[:, ts, vs], ACT.Square, bias=0.25)
            for ts in pairs:
                nc.scalar.activation(inv[h][:, ts, :], sq[h][:, ts, :], ACT.Abs_reciprocal_sqrt)
        for h in range(2):
            vs = slice(h * HALF_V, (h + 1) * HALF_V)
            for t in range(PACK):
                if h == 0 and t % 2 == 0:
                    ts = pairs[t // 2]
                    nc.vector.scalar_tensor_tensor(slack[:, ts, :], mag[:, ts, :], 0.25, rest_sb[:, ts, :], ALU.add, ALU.subtract)
                nc.vector.scalar_tensor_tensor(num[h][:, t, :], nd[:, t, vs], gn_sb[:, t : t + 1], slack[:, t, vs], ALU.mult, ALU.mult)
            nc.vector.tensor_tensor(
                z_bf[h][:].rearrange("p (c i t) -> p c t i", i=4, t=PACK),
                num[h][:].rearrange("p t (c i) -> p c t i", i=4),
                inv[h][:].rearrange("p t (c i) -> p c t i", i=4),
                ALU.mult,
            )
            nc.vector.quantize_mx(out=z_words[h][:].bitcast(FP8X4), scales=z_scales[h][:], in_=z_bf[h][:])

        for h in range(2):
            vs = slice(h * HALF_V, (h + 1) * HALF_V)
            for g in range(2):
                res = sb(f"res{h}{g}", [P, 2, HALF_V], F32)
                for e in range(2):
                    mc = slice((2 * g + e) * P, (2 * g + e + 1) * P)
                    acc = psum.tile([P, HALF_V], F32, name=f"out_acc{h}{g}{e}", tag=f"bank{(2 + 4 * h + 2 * g + e) % 8}")
                    nc.tensor.matmul_mx(out=acc[:], lhsT=w2_words[:, mc].bitcast(FP8X4), lhsT_scale=w2_scales[:, mc], rhs=z_words[h][:].bitcast(FP8X4), rhs_scale=z_scales[h][:], start=True, stop=True)
                    if h == 0 or e == 0:
                        nc.scalar.copy(res[:, e, :], acc[:])
                    else:
                        nc.vector.tensor_copy(res[:, e, :], acc[:])
                nc.sync.dma_start(out_rows[:, 2 * g : 2 * g + 2, vs], res[:])
